import numpy as np
import ml_dtypes


def mxq(x, axis, fmt="e4m3"):
    dtype, down = {"e4m3": (ml_dtypes.float8_e4m3fn, 7), "e5m2": (ml_dtypes.float8_e5m2, 14)}[fmt]
    v = np.moveaxis(np.asarray(x, np.float32).astype(ml_dtypes.bfloat16).astype(np.float64), axis, -1)
    blocks = v.reshape(v.shape[:-1] + (-1, 32))
    amax = np.abs(blocks).max(-1, keepdims=True)
    byte = np.maximum(np.where(amax > 0, np.frexp(amax)[1] - 1 + 127, 0) - down, 1)
    scale = np.exp2(byte - 127.0)
    codes = (blocks / scale).astype(np.float32).astype(dtype).astype(np.float64)
    return np.moveaxis((codes * scale).reshape(v.shape), -1, axis)


WIDE = False


def mx_kscale(k):
    if not WIDE:
        return np.ones(k)
    levels = np.array([10, -10, 5, -5, 0])
    if k % 512:
        return np.exp2(np.random.permutation(np.resize(levels, k // 32))).repeat(32)
    a = np.empty((k // 512, 16))
    for p in range(k // 512):
        a[p, :8] = np.random.permutation(np.resize(levels, 8))
        for g in range(8):
            far = levels[np.abs(levels - a[p, g]) >= 10]
            a[p, g + 8] = far[np.random.randint(len(far))]
    return np.exp2(a.ravel()).repeat(32)


def f64(x):
    return np.asarray(x).astype(np.float64)


def striped(idx):
    return np.tile(idx.reshape(-1, 16).T, (8, 1)).astype(np.uint16)


def unstriped(offs):
    return offs[:16].T.reshape(-1).astype(np.int64)


E2M1 = np.array([0.0, 0.5, 1.0, 1.5, 2.0, 3.0, 4.0, 6.0, -0.0, -0.5, -1.0, -1.5, -2.0, -3.0, -4.0, -6.0])


def pack_weight(w, fmt):
    k, n = w.shape
    w = f64(np.asarray(w, np.float32).astype(ml_dtypes.bfloat16)).reshape(k // 32, 32, n)
    amax = np.abs(w).max(1)
    if fmt == "e4m3":
        byte = np.frexp(amax)[1] - 1 + 127 - 7
    else:
        mant, ex = np.frexp(amax / 6.0)
        byte = np.where(mant > 0.5, ex, ex - 1) + 127
    byte = np.clip(np.where(amax > 0, byte, 1), 1, 254)
    scaled = (w * np.exp2(127.0 - byte)[:, None, :]).reshape(k, n).astype(np.float32)
    by_word = np.ascontiguousarray(scaled.reshape(k // 512, 128, 4, n).transpose(0, 1, 3, 2))
    if fmt == "e4m3":
        words = by_word.astype(ml_dtypes.float8_e4m3fn).view(np.uint8)
    else:
        c = by_word.astype(ml_dtypes.float4_e2m1fn).view(np.uint8) & 0xF
        words = (c[..., 0::2] | (c[..., 1::2] << 4)).reshape(k // 512, 128, 2 * n)
    return np.ascontiguousarray(words), np.ascontiguousarray(byte.astype(np.uint8).reshape(k // 512, 16, n))


def unpack_weight(words, scales, fmt):
    g, _, n = scales.shape
    words = np.ascontiguousarray(words).reshape(g, 128, n, -1)
    if fmt == "e4m3":
        vals = words.view(ml_dtypes.float8_e4m3fn).astype(np.float64)
    else:
        nib = np.empty((g, 128, n, 4), np.uint8)
        nib[..., 0::2] = words & 0xF
        nib[..., 1::2] = words >> 4
        vals = E2M1[nib]
    vals = vals * np.repeat(np.exp2(scales.astype(np.float64) - 127.0), 8, axis=1)[..., None]
    return vals.transpose(0, 1, 3, 2).reshape(g * 512, n)


def gelu(v):
    return 0.5 * v * (1.0 + np.tanh(np.sqrt(2.0 / np.pi) * (v + 0.044715 * v**3)))


T, S, K, KI, H, T2, P, T3, S2 = 2048, 1024, 1024, 512, 512, 2048, 512, 2048, 1024

def setup_inputs():
    n = np.random.standard_normal
    s = mx_kscale(K)[:, None]
    si = mx_kscale(KI)[:, None]
    u = mx_kscale(H)[:, None]
    tab_words, tab_scales = pack_weight(n((K, T)) * s, "e4m3")
    img_words, img_scales = pack_weight(n((KI, S)) * si, "e4m3")
    w3_words, w3_scales = pack_weight(1.4 * n((K, H)) / s / np.sqrt(K), "e2m1")
    tab2_words, tab2_scales = pack_weight(n((H, T3)) / u / np.sqrt(H), "e4m3")
    return {
        "tab_words": tab_words, "tab_scales": tab_scales,
        "offs": striped(np.random.permutation(T)[:S]),
        "img_words": img_words, "img_scales": img_scales,
        "w1": (n((K, H)) / s * u.T / np.sqrt(K)).astype(np.float32),
        "w2": (n((KI, H)) / si * u.T / np.sqrt(KI)).astype(np.float32),
        "w3_words": w3_words, "w3_scales": w3_scales,
        "b3": (0.5 * n(H)).astype(np.float32),
        "page0": (n((H, T2)) * u).astype(np.float32),
        "wgs": np.exp(0.3 * n((128, S))).astype(np.float32),
        "offs3": striped(np.random.permutation(T2)[:S]),
        "offs4": striped(np.random.permutation(T2)[:P]),
        "cap": ((n((H, P)) + 0.3) * u).astype(np.float32),
        "tab2_words": tab2_words, "tab2_scales": tab2_scales,
        "offs2": striped(np.random.permutation(T3)[:S2]),
        "gain": np.exp(0.5 * n(S2)).astype(np.float32),
    }

def reference(tab_words, tab_scales, offs, img_words, img_scales, w1, w2, w3_words, w3_scales, b3, page0, wgs, offs3, offs4, cap, tab2_words, tab2_scales, offs2, gain):
    v = unpack_weight(tab_words, tab_scales, "e4m3")[:, unstriped(offs)]
    img = unpack_weight(img_words, img_scales, "e4m3")
    both = mxq(f64(w1), 0, "e4m3").T @ v + mxq(f64(w2), 0, "e4m3").T @ img
    read = np.tanh((unpack_weight(w3_words, w3_scales, "e2m1").T @ v) + f64(b3)[:, None])
    h = both * read
    page = f64(page0).copy()
    page[:, unstriped(offs3)] = np.tile(f64(wgs), (H // 128, 1)) * h
    x = np.minimum(page[:, unstriped(offs4)], f64(cap))
    v2 = unpack_weight(tab2_words, tab2_scales, "e4m3")[:, unstriped(offs2)]
    e = v2.T @ mxq(x, 0, "e4m3")
    return e * f64(gain)[:, None]

@@ -1,0 +1,244 @@
+from contextlib import ExitStack
+
+import concourse.mybir as mybir
+
+T, S, K, KI, H, T2, PW, T3, S2 = 2048, 1024, 1024, 512, 512, 2048, 512, 2048, 1024
+FLOPS = 2 * S * H * (2 * K + KI) + 2 * S2 * PW * H
+
+F32 = mybir.dt.float32
+BF16 = mybir.dt.bfloat16
+I32 = mybir.dt.int32
+U32 = mybir.dt.uint32
+U16 = mybir.dt.uint16
+U8 = mybir.dt.uint8
+FP8X4 = mybir.dt.float8_e4m3fn_x4
+FP4X4 = mybir.dt.float4_e2m1fn_x4
+MULT = mybir.AluOpType.mult
+MIN = mybir.AluOpType.min
+ACT = mybir.ActivationFunctionType
+
+P = 128
+PACK = 4
+QUADS = 4
+NB = 512
+XH = PW // 2
+
+
+def tile_list_stamp_auction_search_kernel(
+    tc, tab_words, tab_scales, offs, img_words, img_scales, w1, w2, w3_words, w3_scales, b3,
+    page0, wgs, offs3, offs4, cap, tab2_words, tab2_scales, offs2, gain, out,
+):
+    nc = tc.nc
+    with ExitStack() as ctx:
+        keep = ctx.enter_context(tc.tile_pool(name="keep", bufs=1))
+        ring = ctx.enter_context(tc.tile_pool(name="ring", bufs=2))
+        psum = ctx.enter_context(tc.psum_pool(name="psum", bufs=8))
+
+        def new(shape, dtype, name):
+            return keep.tile(shape, dtype, name=name, align_bytes=64)
+
+        def load_list(src, name):
+            dst = new([P, src.shape[1]], U16, name)
+            nc.sync.dma_start(dst[:], src)
+            return dst
+
+        def load_words(src, name):
+            dst = new([P, src.shape[1]], I32, name)
+            nc.sync.dma_start(dst[:], src.rearrange("p c i -> p (c i)").bitcast(I32))
+            return dst
+
+        def zeroed(width, name):
+            dst = new([P, width], U8, name)
+            nc.vector.memset(dst[:].bitcast(I32), 0)
+            return dst
+
+        def gather(src, dtype, offsets, name):
+            dst = new([P, 16 * offsets.shape[1]], dtype, name)
+            nc.vector.tensor_copy(dst[:], src.indirect(offsets[:]))
+            return dst
+
+        def load_weight(rows, name):
+            raw = new([P, PACK, H], F32, name)
+            nc.sync.dma_start(raw[:], rows.rearrange("(p j) c -> p j c", j=PACK))
+            return raw
+
+        def round_weight(raw, name):
+            dst = new([P, PACK * H], BF16, name)
+            nc.scalar.copy(
+                dst[:].rearrange("p (t m j) -> p m j t", t=PACK, j=PACK),
+                raw[:].rearrange("p j (m t) -> p m j t", t=PACK),
+            )
+            return dst
+
+        def quantize(src, width, name):
+            codes = new([P, width], U32, name + "_codes")
+            scales = new([P, width], U8, name + "_scales")
+            nc.vector.quantize_mx(out=codes[:].bitcast(FP8X4), scales=scales[:], in_=src)
+            return codes, scales
+
+        tab_sc = zeroed(T, "tab_sc")
+        w3_sc = zeroed(2 * H, "w3_sc")
+        tab2_sc = zeroed(T3, "tab2_sc")
+        img_sc = zeroed(S, "img_sc")
+        v_sc1 = zeroed(S, "v_sc1")
+
+        idx = load_list(offs, "idx")
+        tab_w0 = load_words(tab_words[0], "tab_w0")
+        for q in range(QUADS):
+            nc.sync.dma_start(
+                tab_sc[32 * q : 32 * q + 8, :].bitcast(I32),
+                tab_scales[:, 4 * q : 4 * q + 4, :].bitcast(I32),
+            )
+        w1_raw0 = load_weight(w1[0:512, :], "w1_raw0")
+        w3_w = new([P, 2, 2 * H], U8, "w3_w")
+        nc.sync.dma_start(w3_w[:].bitcast(I32), w3_words.rearrange("a p n -> p a n").bitcast(I32))
+        for q in range(QUADS):
+            nc.sync.dma_start(
+                w3_sc[32 * q : 32 * q + 4, :].bitcast(I32).rearrange("r (a n) -> r a n", a=2),
+                w3_scales[:, 4 * q : 4 * q + 4, :].bitcast(I32).rearrange("a r n -> r a n"),
+            )
+        tab_w1 = load_words(tab_words[1], "tab_w1")
+        w1_raw1 = load_weight(w1[512:1024, :], "w1_raw1")
+        idx2 = load_list(offs2, "idx2")
+        for q in range(QUADS):
+            nc.sync.dma_start(
+                tab2_sc[32 * q : 32 * q + 4, :].bitcast(I32),
+                tab2_scales[0, 4 * q : 4 * q + 4, :].bitcast(I32),
+            )
+        w2_raw = load_weight(w2, "w2_raw")
+        img_w = load_words(img_words[0], "img_w")
+        bias = new([P, PACK], F32, "bias")
+        nc.sync.dma_start(bias[:], b3.rearrange("(p t) -> p t", t=PACK))
+        for q in range(QUADS):
+            nc.sync.dma_start(
+                img_sc[32 * q : 32 * q + 4, :].bitcast(I32),
+                img_scales[0, 4 * q : 4 * q + 4, :].bitcast(I32),
+            )
+        wgs_rows = wgs.rearrange("(q t) j -> q t j", t=PACK)
+        page_rows = page0.rearrange("(p t) c -> p t c", t=PACK)
+        wg_first = new([P, S], F32, "wg_first")
+        for q in range(QUADS):
+            nc.sync.dma_start(wg_first[32 * q : 32 * q + 32, :], wgs_rows[:, 0, :])
+        idx3 = load_list(offs3, "idx3")
+        pages = [new([P, T2], F32, "page%d" % t) for t in range(PACK)]
+        nc.sync.dma_start(pages[0][:], page_rows[:, 0, :])
+        tab2_w = load_words(tab2_words[0], "tab2_w")
+        wg_rest = new([P, PACK - 1, S], F32, "wg_rest")
+        for q in range(QUADS):
+            nc.sync.dma_start(wg_rest[32 * q : 32 * q + 32, :, :], wgs_rows[:, 1:PACK, :])
+        nc.sync.dma_start(pages[1][:], page_rows[:, 1, :])
+        idx4 = load_list(offs4, "idx4")
+        nc.sync.dma_start(pages[2][:], page_rows[:, 2, :])
+        nc.sync.dma_start(pages[3][:], page_rows[:, 3, :])
+        caps = new([P, PACK, PW], F32, "caps")
+        nc.sync.dma_start(caps[:], cap.rearrange("(p t) j -> p t j", t=PACK))
+        gains = new([P, S2 // P], F32, "gains")
+        with nc.allow_non_contiguous_dma(reason="one gain a partition"):
+            nc.sync.dma_start(gains[:], gain.rearrange("(b p) -> p b", p=P))
+        wg = [wg_first[:]] + [wg_rest[:, t, :] for t in range(PACK - 1)]
+
+        v_w0 = gather(tab_w0[:].bitcast(U32), U32, idx, "v_w0")
+        v_sc0 = gather(tab_sc[:], U8, idx, "v_sc0")
+        nc.gpsimd.dma_start(v_sc1[0 : P - 4, :].bitcast(I32), v_sc0[4:P, :].bitcast(I32))
+        w1_bf0 = round_weight(w1_raw0, "w1_bf0")
+        w3_dw = new([P, 2, 2 * H], U8, "w3_dw")
+        nc.vector.tensor_copy(
+            w3_dw[:].bitcast(U16).rearrange("p a (t m) -> p a t m", t=PACK),
+            w3_w[:].bitcast(U16).rearrange("p a (m t) -> p a t m", t=PACK),
+        )
+        w3_ds = new([P, 2, H], U8, "w3_ds")
+        nc.vector.tensor_copy(
+            w3_ds[:].rearrange("p a (t m) -> p a t m", t=PACK),
+            w3_sc[:].rearrange("p (a m t) -> p a t m", a=2, t=PACK),
+        )
+        v_w1 = gather(tab_w1[:].bitcast(U32), U32, idx, "v_w1")
+        w1_q0 = quantize(w1_bf0[:], H, "w1_q0")
+        w1_bf1 = round_weight(w1_raw1, "w1_bf1")
+        v2_sc = gather(tab2_sc[:], U8, idx2, "v2_sc")
+        w1_q1 = quantize(w1_bf1[:], H, "w1_q1")
+        w2_bf = round_weight(w2_raw, "w2_bf")
+        w2_q = quantize(w2_bf[:], H, "w2_q")
+
+        v = [(v_w0, v_sc0), (v_w1, v_sc1)]
+        both_passes = [(w1_q0, v[0]), (w1_q1, v[1]), (w2_q, (img_w, img_sc))]
+
+        def reading(t):
+            h = ring.tile([P, S], F32, name="h")
+            rows = slice(P * t, P * (t + 1))
+            for n0 in range(0, S, NB):
+                cols = slice(n0, n0 + NB)
+                z = psum.tile([P, NB], F32, name="acc")
+                for a in range(2):
+                    nc.tensor.matmul_mx(
+                        out=z[:],
+                        lhsT=w3_dw[:, a, 2 * P * t : 2 * P * (t + 1)].bitcast(FP4X4),
+                        lhsT_scale=w3_ds[:, a, rows],
+                        rhs=v[a][0][:, cols].bitcast(FP8X4),
+                        rhs_scale=v[a][1][:, cols],
+                        start=(a == 0),
+                        stop=(a == 1),
+                    )
+                read = ring.tile([P, NB], F32, name="read", bufs=4)
+                nc.scalar.activation(read[:], z[:], ACT.Tanh, bias=bias[:, t : t + 1])
+                both = psum.tile([P, NB], F32, name="acc")
+                for a, (w_q, moving) in enumerate(both_passes):
+                    nc.tensor.matmul_mx(
+                        out=both[:],
+                        lhsT=w_q[0][:, rows].bitcast(FP8X4),
+                        lhsT_scale=w_q[1][:, rows],
+                        rhs=moving[0][:, cols].bitcast(FP8X4),
+                        rhs_scale=moving[1][:, cols],
+                        start=(a == 0),
+                        stop=(a == len(both_passes) - 1),
+                    )
+                nc.vector.tensor_tensor(h[:, cols], both[:], read[:], MULT)
+            return h
+
+        picked = new([P, PACK, PW], F32, "picked")
+        h = reading(0)
+        for t in range(PACK):
+            nc.vector.tensor_tensor(pages[t][:].indirect(idx3[:]), h[:], wg[t], MULT)
+            if t == 0:
+                v2_w = gather(tab2_w[:].bitcast(U32), U32, idx2, "v2_w")
+            if t + 1 < PACK:
+                h = reading(t + 1)
+                nc.vector.tensor_copy(picked[:, t, :], pages[t][:].indirect(idx4[:]))
+        last = PACK - 1
+        for half in range(2):
+            nc.vector.tensor_copy(
+                picked[:, last, XH * half : XH * (half + 1)],
+                pages[last][:].indirect(idx4[:, XH // 16 * half : XH // 16 * (half + 1)]),
+            )
+
+        out_rows = out.rearrange("(b p) j -> p b j", p=P)
+        for half in range(2):
+            cols = slice(XH * half, XH * (half + 1))
+            x = new([P, XH, PACK], BF16, "x%d" % half)
+            nc.vector.tensor_tensor(
+                x[:].rearrange("p (c i) t -> p c t i", i=4),
+                picked[:, :, cols].rearrange("p t (c i) -> p c t i", i=4),
+                caps[:, :, cols].rearrange("p t (c i) -> p c t i", i=4),
+                MIN,
+            )
+            x_codes, x_scales = quantize(x[:].rearrange("p c t -> p (c t)"), XH, "x_q%d" % half)
+            for pair in range(S2 // P // 2):
+                e = psum.tile([P, 2, XH], F32, name="acc")
+                for u in range(2):
+                    lots = slice(P * (2 * pair + u), P * (2 * pair + u + 1))
+                    nc.tensor.matmul_mx(
+                        out=e[:, u, :],
+                        lhsT=v2_w[:, lots].bitcast(FP8X4),
+                        lhsT_scale=v2_sc[:, lots],
+                        rhs=x_codes[:].bitcast(FP8X4),
+                        rhs_scale=x_scales[:],
+                        start=True,
+                        stop=True,
+                    )
+                staged = ring.tile([P, 2, XH], F32, name="staged", bufs=8)
+                for u in range(2):
+                    g = gains[:, 2 * pair + u : 2 * pair + u + 1]
+                    if half == 1 and pair < 3:
+                        nc.vector.tensor_scalar(staged[:, u, :], e[:, u, :], g, None, MULT)
+                    else:
+                        nc.scalar.activation(staged[:, u, :], e[:, u, :], ACT.Copy, scale=g)
+                nc.sync.dma_start(out_rows[:, 2 * pair : 2 * pair + 2, cols], staged[:])

@@ -1,6 +1,7 @@
 from contextlib import ExitStack
 
 import concourse.mybir as mybir
+from concourse.masks import make_identity
 
 T, S, K, KI, H, T2, PW, T3, S2 = 2048, 1024, 1024, 512, 512, 2048, 512, 2048, 1024
 FLOPS = 2 * S * H * (2 * K + KI) + 2 * S2 * PW * H
@@ -21,7 +22,11 @@ P = 128
 PACK = 4
 QUADS = 4
 NB = 512
+SLICES = H // P
 XH = PW // 2
+JB = XH // P
+IMG_ROW = 8
+TAB2_ROW = 12
 
 
 def tile_list_stamp_auction_search_kernel(
@@ -32,43 +37,35 @@ def tile_list_stamp_auction_search_kernel(
     with ExitStack() as ctx:
         keep = ctx.enter_context(tc.tile_pool(name="keep", bufs=1))
         ring = ctx.enter_context(tc.tile_pool(name="ring", bufs=2))
-        psum = ctx.enter_context(tc.psum_pool(name="psum", bufs=8))
+        once = ctx.enter_context(tc.tile_pool(name="once", bufs=1))
+        psum = ctx.enter_context(tc.psum_pool(name="psum", bufs=2))
 
         def new(shape, dtype, name):
             return keep.tile(shape, dtype, name=name, align_bytes=64)
 
-        def load_list(src, name):
-            dst = new([P, src.shape[1]], U16, name)
+        def load(src, name):
+            dst = new(list(src.shape), src.dtype, name)
             nc.sync.dma_start(dst[:], src)
             return dst
 
         def load_words(src, name):
-            dst = new([P, src.shape[1]], I32, name)
-            nc.sync.dma_start(dst[:], src.rearrange("p c i -> p (c i)").bitcast(I32))
-            return dst
+            return load(src.rearrange("p c i -> p (c i)").bitcast(I32), name)
 
         def zeroed(width, name):
             dst = new([P, width], U8, name)
             nc.vector.memset(dst[:].bitcast(I32), 0)
             return dst
 
-        def gather(src, dtype, offsets, name):
-            dst = new([P, 16 * offsets.shape[1]], dtype, name)
-            nc.vector.tensor_copy(dst[:], src.indirect(offsets[:]))
-            return dst
+        def load_scales(dst, src, row):
+            for q in range(QUADS):
+                rows = dst[32 * q + row : 32 * q + row + 4, :].bitcast(I32)
+                nc.sync.dma_start(
+                    rows.rearrange("r (a n) -> r a n", a=src.shape[0]),
+                    src[:, 4 * q : 4 * q + 4, :].bitcast(I32).rearrange("a r n -> r a n"),
+                )
 
-        def load_weight(rows, name):
-            raw = new([P, PACK, H], F32, name)
-            nc.sync.dma_start(raw[:], rows.rearrange("(p j) c -> p j c", j=PACK))
-            return raw
-
-        def round_weight(raw, name):
-            dst = new([P, PACK * H], BF16, name)
-            nc.scalar.copy(
-                dst[:].rearrange("p (t m j) -> p m j t", t=PACK, j=PACK),
-                raw[:].rearrange("p j (m t) -> p m j t", t=PACK),
-            )
-            return dst
+        def gather(dst, window, offsets):
+            nc.vector.tensor_copy(dst, window.indirect(offsets))
 
         def quantize(src, width, name):
             codes = new([P, width], U32, name + "_codes")
@@ -76,159 +73,180 @@ def tile_list_stamp_auction_search_kernel(
             nc.vector.quantize_mx(out=codes[:].bitcast(FP8X4), scales=scales[:], in_=src)
             return codes, scales
 
-        tab_sc = zeroed(T, "tab_sc")
+        def load_weight(rows, cols, name):
+            return load(rows.rearrange("(p i) c -> p i c", i=PACK)[:, :, cols], name)
+
+        def quantize_weights(raws, rounded, name):
+            quantized = []
+            for a, raw in enumerate(raws):
+                nc.scalar.copy(
+                    rounded[a].rearrange("p (c i) -> p c i", i=PACK),
+                    raw[:].rearrange("p i c -> p c i"),
+                )
+                quantized.append(quantize(rounded[a], raw.shape[2], "%s%d" % (name, a)))
+            return quantized
+
+        def turn_bank(shape):
+            return psum.tile(shape, F32, name="turn", bufs=4)
+
+        def turned(src, dst):
+            blocks = dst.shape[1]
+            for b in range(blocks):
+                nc.tensor.transpose(dst[:, b, :], src[:, P * b : P * (b + 1)], ident[:])
+            return dst
+
+        ident = new([P, P], F32, "ident")
+        make_identity(nc, ident[:])
+        tab_sc = zeroed(2 * T, "tab_sc")
         w3_sc = zeroed(2 * H, "w3_sc")
-        tab2_sc = zeroed(T3, "tab2_sc")
         img_sc = zeroed(S, "img_sc")
-        v_sc1 = zeroed(S, "v_sc1")
+        tab2_sc = zeroed(T3, "tab2_sc")
 
-        idx = load_list(offs, "idx")
+        w_passes = [w1[0:512, :], w2, w1[512:1024, :]]
+        first_cols, rest_cols = slice(0, P), slice(P, H)
+        page_rows = page0.rearrange("(s p) c -> s p c", p=P)
+
+        idx = load(offs, "idx")
         tab_w0 = load_words(tab_words[0], "tab_w0")
-        for q in range(QUADS):
-            nc.sync.dma_start(
-                tab_sc[32 * q : 32 * q + 8, :].bitcast(I32),
-                tab_scales[:, 4 * q : 4 * q + 4, :].bitcast(I32),
-            )
-        w1_raw0 = load_weight(w1[0:512, :], "w1_raw0")
-        w3_w = new([P, 2, 2 * H], U8, "w3_w")
-        nc.sync.dma_start(w3_w[:].bitcast(I32), w3_words.rearrange("a p n -> p a n").bitcast(I32))
-        for q in range(QUADS):
-            nc.sync.dma_start(
-                w3_sc[32 * q : 32 * q + 4, :].bitcast(I32).rearrange("r (a n) -> r a n", a=2),
-                w3_scales[:, 4 * q : 4 * q + 4, :].bitcast(I32).rearrange("a r n -> r a n"),
-            )
+        load_scales(tab_sc, tab_scales, 0)
+        raw_first = [load_weight(w_passes[a], first_cols, "raw_first%d" % a) for a in range(2)]
+        w3_w = load(w3_words.rearrange("a p n -> p a n").bitcast(I32), "w3_w")
+        load_scales(w3_sc, w3_scales, 0)
+        raw_first.append(load_weight(w_passes[2], first_cols, "raw_first2"))
         tab_w1 = load_words(tab_words[1], "tab_w1")
-        w1_raw1 = load_weight(w1[512:1024, :], "w1_raw1")
-        idx2 = load_list(offs2, "idx2")
-        for q in range(QUADS):
-            nc.sync.dma_start(
-                tab2_sc[32 * q : 32 * q + 4, :].bitcast(I32),
-                tab2_scales[0, 4 * q : 4 * q + 4, :].bitcast(I32),
-            )
-        w2_raw = load_weight(w2, "w2_raw")
         img_w = load_words(img_words[0], "img_w")
-        bias = new([P, PACK], F32, "bias")
-        nc.sync.dma_start(bias[:], b3.rearrange("(p t) -> p t", t=PACK))
-        for q in range(QUADS):
-            nc.sync.dma_start(
-                img_sc[32 * q : 32 * q + 4, :].bitcast(I32),
-                img_scales[0, 4 * q : 4 * q + 4, :].bitcast(I32),
-            )
-        wgs_rows = wgs.rearrange("(q t) j -> q t j", t=PACK)
-        page_rows = page0.rearrange("(p t) c -> p t c", t=PACK)
-        wg_first = new([P, S], F32, "wg_first")
-        for q in range(QUADS):
-            nc.sync.dma_start(wg_first[32 * q : 32 * q + 32, :], wgs_rows[:, 0, :])
-        idx3 = load_list(offs3, "idx3")
-        pages = [new([P, T2], F32, "page%d" % t) for t in range(PACK)]
-        nc.sync.dma_start(pages[0][:], page_rows[:, 0, :])
+        with nc.allow_non_contiguous_dma(reason="one value a partition"):
+            bias = load(b3.rearrange("(s p) -> p s", p=P), "bias")
+        load_scales(img_sc, img_scales, IMG_ROW)
+        wg = load(wgs, "wg")
+        pages = [load(page_rows[0], "page0")]
+        idx3 = load(offs3, "idx3")
+        idx4 = load(offs4, "idx4")
+        idx2 = load(offs2, "idx2")
+        raw_rest = [load_weight(rows, rest_cols, "raw_rest%d" % a) for a, rows in enumerate(w_passes)]
+        load_scales(tab2_sc, tab2_scales, TAB2_ROW)
         tab2_w = load_words(tab2_words[0], "tab2_w")
-        wg_rest = new([P, PACK - 1, S], F32, "wg_rest")
-        for q in range(QUADS):
-            nc.sync.dma_start(wg_rest[32 * q : 32 * q + 32, :, :], wgs_rows[:, 1:PACK, :])
-        nc.sync.dma_start(pages[1][:], page_rows[:, 1, :])
-        idx4 = load_list(offs4, "idx4")
-        nc.sync.dma_start(pages[2][:], page_rows[:, 2, :])
-        nc.sync.dma_start(pages[3][:], page_rows[:, 3, :])
-        caps = new([P, PACK, PW], F32, "caps")
-        nc.sync.dma_start(caps[:], cap.rearrange("(p t) j -> p t j", t=PACK))
-        gains = new([P, S2 // P], F32, "gains")
-        with nc.allow_non_contiguous_dma(reason="one gain a partition"):
-            nc.sync.dma_start(gains[:], gain.rearrange("(b p) -> p b", p=P))
-        wg = [wg_first[:]] + [wg_rest[:, t, :] for t in range(PACK - 1)]
+        caps = load(cap.rearrange("(s p) j -> p s j", p=P), "caps")
+        for s in range(1, SLICES):
+            pages.append(load(page_rows[s], "page%d" % s))
+        with nc.allow_non_contiguous_dma(reason="one value a partition"):
+            gains = load(gain.rearrange("(b p) -> p b", p=P), "gains")
 
-        v_w0 = gather(tab_w0[:].bitcast(U32), U32, idx, "v_w0")
-        v_sc0 = gather(tab_sc[:], U8, idx, "v_sc0")
-        nc.gpsimd.dma_start(v_sc1[0 : P - 4, :].bitcast(I32), v_sc0[4:P, :].bitcast(I32))
-        w1_bf0 = round_weight(w1_raw0, "w1_bf0")
-        w3_dw = new([P, 2, 2 * H], U8, "w3_dw")
-        nc.vector.tensor_copy(
-            w3_dw[:].bitcast(U16).rearrange("p a (t m) -> p a t m", t=PACK),
-            w3_w[:].bitcast(U16).rearrange("p a (m t) -> p a t m", t=PACK),
-        )
-        w3_ds = new([P, 2, H], U8, "w3_ds")
-        nc.vector.tensor_copy(
-            w3_ds[:].rearrange("p a (t m) -> p a t m", t=PACK),
-            w3_sc[:].rearrange("p (a m t) -> p a t m", a=2, t=PACK),
-        )
-        v_w1 = gather(tab_w1[:].bitcast(U32), U32, idx, "v_w1")
-        w1_q0 = quantize(w1_bf0[:], H, "w1_q0")
-        w1_bf1 = round_weight(w1_raw1, "w1_bf1")
-        v2_sc = gather(tab2_sc[:], U8, idx2, "v2_sc")
-        w1_q1 = quantize(w1_bf1[:], H, "w1_q1")
-        w2_bf = round_weight(w2_raw, "w2_bf")
-        w2_q = quantize(w2_bf[:], H, "w2_q")
+        v_w0 = new([P, S], U32, "v_w0")
+        gather(v_w0[:], tab_w0[:].bitcast(U32), idx[:])
+        v_sc = new([P, 2, S], U8, "v_sc")
+        for a in range(2):
+            gather(v_sc[:, a, :], tab_sc[:, T * a : T * (a + 1)], idx[:])
+        first_bf16 = [new([P, P * PACK], BF16, "first_bf16_%d" % a)[:] for a in range(len(w_passes))]
+        w_first = quantize_weights(raw_first, first_bf16, "w_first")
+        v_w1 = new([P, S], U32, "v_w1")
+        for n0 in range(0, S, NB):
+            gather(v_w1[:, n0 : n0 + NB], tab_w1[:].bitcast(U32), idx[:, n0 // 16 : (n0 + NB) // 16])
 
-        v = [(v_w0, v_sc0), (v_w1, v_sc1)]
-        both_passes = [(w1_q0, v[0]), (w1_q1, v[1]), (w2_q, (img_w, img_sc))]
+        v = [(v_w0, v_sc[:, 0, :]), (v_w1, v_sc[:, 1, :])]
+        moving = [v[0], (img_w, img_sc[IMG_ROW:P, :]), v[1]]
 
-        def reading(t):
-            h = ring.tile([P, S], F32, name="h")
-            rows = slice(P * t, P * (t + 1))
+        def reading(s, weights, w_cols):
+            h = once.tile([P, S], F32, name="h")
             for n0 in range(0, S, NB):
                 cols = slice(n0, n0 + NB)
-                z = psum.tile([P, NB], F32, name="acc")
+                z = psum.tile([P, NB], F32, name="z")
                 for a in range(2):
                     nc.tensor.matmul_mx(
                         out=z[:],
-                        lhsT=w3_dw[:, a, 2 * P * t : 2 * P * (t + 1)].bitcast(FP4X4),
-                        lhsT_scale=w3_ds[:, a, rows],
+                        lhsT=w3_w[:, a, P // 2 * s : P // 2 * (s + 1)].bitcast(FP4X4),
+                        lhsT_scale=w3_sc[:, H * a + P * s : H * a + P * (s + 1)],
                         rhs=v[a][0][:, cols].bitcast(FP8X4),
                         rhs_scale=v[a][1][:, cols],
                         start=(a == 0),
                         stop=(a == 1),
                     )
-                read = ring.tile([P, NB], F32, name="read", bufs=4)
-                nc.scalar.activation(read[:], z[:], ACT.Tanh, bias=bias[:, t : t + 1])
-                both = psum.tile([P, NB], F32, name="acc")
-                for a, (w_q, moving) in enumerate(both_passes):
+                read = once.tile([P, NB], F32, name="read%d" % (n0 // NB), align_bytes=64)
+                nc.scalar.activation(read[:], z[:], ACT.Tanh, bias=bias[:, s : s + 1])
+                both = psum.tile([P, NB], F32, name="both")
+                for a in range(len(moving)):
                     nc.tensor.matmul_mx(
                         out=both[:],
-                        lhsT=w_q[0][:, rows].bitcast(FP8X4),
-                        lhsT_scale=w_q[1][:, rows],
-                        rhs=moving[0][:, cols].bitcast(FP8X4),
-                        rhs_scale=moving[1][:, cols],
+                        lhsT=weights[a][0][:, w_cols].bitcast(FP8X4),
+                        lhsT_scale=weights[a][1][:, w_cols],
+                        rhs=moving[a][0][:, cols].bitcast(FP8X4),
+                        rhs_scale=moving[a][1][:, cols],
                         start=(a == 0),
-                        stop=(a == len(both_passes) - 1),
+                        stop=(a == len(moving) - 1),
                     )
                 nc.vector.tensor_tensor(h[:, cols], both[:], read[:], MULT)
             return h
 
-        picked = new([P, PACK, PW], F32, "picked")
-        h = reading(0)
-        for t in range(PACK):
-            nc.vector.tensor_tensor(pages[t][:].indirect(idx3[:]), h[:], wg[t], MULT)
-            if t == 0:
-                v2_w = gather(tab2_w[:].bitcast(U32), U32, idx2, "v2_w")
-            if t + 1 < PACK:
-                h = reading(t + 1)
-                nc.vector.tensor_copy(picked[:, t, :], pages[t][:].indirect(idx4[:]))
-        last = PACK - 1
-        for half in range(2):
-            nc.vector.tensor_copy(
-                picked[:, last, XH * half : XH * (half + 1)],
-                pages[last][:].indirect(idx4[:, XH // 16 * half : XH // 16 * (half + 1)]),
+        caps_t = new([P, SLICES, PW // P, P], F32, "caps_t")
+        x_t = [new([P, JB, H], BF16, "x_t%d" % half) for half in range(2)]
+
+        def pick(s, b0, picked):
+            blocks = picked.shape[1] // P
+            gather(picked[:], pages[s][:], idx4[:, P // 16 * b0 : P // 16 * (b0 + blocks)])
+            return turned(picked, turn_bank([P, blocks, P]))
+
+        def capped(s, half, picked_t):
+            nc.vector.tensor_tensor(
+                x_t[half][:, :, P * s : P * (s + 1)],
+                picked_t,
+                caps_t[:, s, JB * half : JB * (half + 1), :],
+                MIN,
             )
+
+        h = reading(0, w_first, first_cols)
+        last = SLICES - 1
+
+        def turn_caps(s):
+            bank = psum.tile([P, PW // P, P], F32, name="both")
+            nc.scalar.copy(caps_t[:, s, :, :], turned(caps[:, s, :], bank)[:])
+
+        picked_t = None
+        for s in range(last):
+            nc.vector.tensor_tensor(pages[s][:].indirect(idx3[:]), h[:], wg[:], MULT)
+            if s == 0:
+                rest_bf16 = once.tile([P, len(w_passes), (H - P) * PACK], BF16, name="read1", align_bytes=64)
+                w_rest = quantize_weights(raw_rest, [rest_bf16[:, a, :] for a in range(len(w_passes))], "w_rest")
+                v2_sc = new([P, S2], U8, "raw_rest0")
+                gather(v2_sc[:], tab2_sc[:], idx2[:])
+                v2_w = new([P, S2], U32, "raw_rest2")
+                gather(v2_w[:], tab2_w[:].bitcast(U32), idx2[:])
+            else:
+                for half in range(2):
+                    capped(s - 1, half, picked_t[:, JB * half : JB * (half + 1), :])
+            h = reading(s + 1, w_rest, slice(P * s, P * (s + 1)))
+            turn_caps(s)
+            picked_t = pick(s, 0, once.tile([P, PW], F32, name="read1", align_bytes=64))
+        turn_caps(last)
+        nc.vector.tensor_tensor(pages[last][:].indirect(idx3[:]), h[:], wg[:], MULT)
+        picked_last = [pick(last, JB * half, new([P, XH], F32, "picked%d" % half)) for half in range(2)]
+        for half in range(2):
+            capped(last - 1, half, picked_t[:, JB * half : JB * (half + 1), :])
+        for half in range(2):
+            capped(last, half, picked_last[half][:])
 
         out_rows = out.rearrange("(b p) j -> p b j", p=P)
         for half in range(2):
             cols = slice(XH * half, XH * (half + 1))
-            x = new([P, XH, PACK], BF16, "x%d" % half)
-            nc.vector.tensor_tensor(
-                x[:].rearrange("p (c i) t -> p c t i", i=4),
-                picked[:, :, cols].rearrange("p t (c i) -> p c t i", i=4),
-                caps[:, :, cols].rearrange("p t (c i) -> p c t i", i=4),
-                MIN,
+            pairs = turn_bank([P, JB, 2, P])
+            for b in range(JB):
+                words = x_t[half][:, b, :].bitcast(F32)
+                for u in range(2):
+                    nc.tensor.transpose(pairs[:, b, u, :], words[:, u : H // 2 : 2], ident[:])
+            x = new([P, XH * PACK], BF16, "x%d" % half)
+            weave = nc.scalar.copy if half == 0 else nc.vector.tensor_copy
+            weave(
+                x[:].bitcast(F32).rearrange("p (b j u) -> p b j u", b=JB, u=2),
+                pairs[:].rearrange("p b u j -> p b j u"),
             )
-            x_codes, x_scales = quantize(x[:].rearrange("p c t -> p (c t)"), XH, "x_q%d" % half)
+            x_codes, x_scales = quantize(x[:], XH, "x_q%d" % half)
             for pair in range(S2 // P // 2):
-                e = psum.tile([P, 2, XH], F32, name="acc")
+                e = psum.tile([P, 2, XH], F32, name=("z", "both")[pair % 2])
                 for u in range(2):
                     lots = slice(P * (2 * pair + u), P * (2 * pair + u + 1))
                     nc.tensor.matmul_mx(
                         out=e[:, u, :],
                         lhsT=v2_w[:, lots].bitcast(FP8X4),
-                        lhsT_scale=v2_sc[:, lots],
+                        lhsT_scale=v2_sc[TAB2_ROW:P, lots],
                         rhs=x_codes[:].bitcast(FP8X4),
                         rhs_scale=x_scales[:],
                         start=True,

@@ -134,56 +134,73 @@ def tile_list_stamp_auction_search_kernel(
 
         v_w0 = new([P, S], U32, "v_w0")
         gather(v_w0[:], tab_w0[:].bitcast(U32), idx[:])
-        v_sc = new([P, 2, S], U8, "v_sc")
-        for a in range(2):
-            gather(v_sc[:, a, :], tab_sc[:, T * a : T * (a + 1)], idx[:])
+        v_sc0 = new([P, S], U8, "v_sc0")
+        gather(v_sc0[:], tab_sc[:, 0:T], idx[:])
         first_bf16 = [new([P, P * PACK], BF16, "first_bf16_%d" % a)[:] for a in range(len(w_passes))]
         w_first = quantize_weights(raw_first, first_bf16, "w_first")
+        v_sc1 = new([P, S], U8, "first_bf16_1")
+        gather(v_sc1[:], tab_sc[:, T : 2 * T], idx[:])
         v_w1 = new([P, S], U32, "v_w1")
         for n0 in range(0, S, NB):
             gather(v_w1[:, n0 : n0 + NB], tab_w1[:].bitcast(U32), idx[:, n0 // 16 : (n0 + NB) // 16])
 
-        v = [(v_w0, v_sc[:, 0, :]), (v_w1, v_sc[:, 1, :])]
+        v = [(v_w0, v_sc0), (v_w1, v_sc1)]
         moving = [v[0], (img_w, img_sc[IMG_ROW:P, :]), v[1]]
 
-        def reading(s, weights, w_cols):
-            h = once.tile([P, S], F32, name="h")
-            for n0 in range(0, S, NB):
-                cols = slice(n0, n0 + NB)
-                z = psum.tile([P, NB], F32, name="z")
-                for a in range(2):
-                    nc.tensor.matmul_mx(
-                        out=z[:],
-                        lhsT=w3_w[:, a, P // 2 * s : P // 2 * (s + 1)].bitcast(FP4X4),
-                        lhsT_scale=w3_sc[:, H * a + P * s : H * a + P * (s + 1)],
-                        rhs=v[a][0][:, cols].bitcast(FP8X4),
-                        rhs_scale=v[a][1][:, cols],
-                        start=(a == 0),
-                        stop=(a == 1),
-                    )
-                read = once.tile([P, NB], F32, name="read%d" % (n0 // NB), align_bytes=64)
-                nc.scalar.activation(read[:], z[:], ACT.Tanh, bias=bias[:, s : s + 1])
-                both = psum.tile([P, NB], F32, name="both")
-                for a in range(len(moving)):
-                    nc.tensor.matmul_mx(
-                        out=both[:],
-                        lhsT=weights[a][0][:, w_cols].bitcast(FP8X4),
-                        lhsT_scale=weights[a][1][:, w_cols],
-                        rhs=moving[a][0][:, cols].bitcast(FP8X4),
-                        rhs_scale=moving[a][1][:, cols],
-                        start=(a == 0),
-                        stop=(a == len(moving) - 1),
-                    )
-                nc.vector.tensor_tensor(h[:, cols], both[:], read[:], MULT)
-            return h
+        halves = [slice(n0, n0 + NB) for n0 in range(0, S, NB)]
+
+        def tanh_part(s, cols, read):
+            z = psum.tile([P, NB], F32, name="z")
+            for a in range(2):
+                nc.tensor.matmul_mx(
+                    out=z[:],
+                    lhsT=w3_w[:, a, P // 2 * s : P // 2 * (s + 1)].bitcast(FP4X4),
+                    lhsT_scale=w3_sc[:, H * a + P * s : H * a + P * (s + 1)],
+                    rhs=v[a][0][:, cols].bitcast(FP8X4),
+                    rhs_scale=v[a][1][:, cols],
+                    start=(a == 0),
+                    stop=(a == 1),
+                )
+            nc.scalar.activation(read, z[:], ACT.Tanh, bias=bias[:, s : s + 1])
+
+        def sum_part(weights, w_cols, cols):
+            both = psum.tile([P, NB], F32, name="both")
+            for a in range(len(moving)):
+                nc.tensor.matmul_mx(
+                    out=both[:],
+                    lhsT=weights[a][0][:, w_cols].bitcast(FP8X4),
+                    lhsT_scale=weights[a][1][:, w_cols],
+                    rhs=moving[a][0][:, cols].bitcast(FP8X4),
+                    rhs_scale=moving[a][1][:, cols],
+                    start=(a == 0),
+                    stop=(a == len(moving) - 1),
+                )
+            return both
+
+        def weighted_read(s):
+            read = new([P, S], F32, "read_s%d" % s)
+            weighted = new([P, S], F32, "weighted%d" % s)
+            for cols in halves:
+                tanh_part(s, cols, read[:, cols])
+                nc.gpsimd.tensor_tensor(weighted[:, cols], read[:, cols], wg[:, cols], MULT)
+            return weighted
+
+        def copied_sum(s):
+            dst = new([P, S], F32, "sum%d" % s)
+            for cols in halves:
+                nc.scalar.copy(dst[:, cols], sum_part(w_rest, slice(P * (s - 1), P * s), cols)[:])
+            return dst
 
         caps_t = new([P, SLICES, PW // P, P], F32, "caps_t")
         x_t = [new([P, JB, H], BF16, "x_t%d" % half) for half in range(2)]
 
-        def pick(s, b0, picked):
-            blocks = picked.shape[1] // P
+        def pick(s, b0, picked, bank):
+            blocks = bank.shape[1]
             gather(picked[:], pages[s][:], idx4[:, P // 16 * b0 : P // 16 * (b0 + blocks)])
-            return turned(picked, turn_bank([P, blocks, P]))
+            return turned(picked, bank)
+
+        def pick_whole(s, bank):
+            return pick(s, 0, ring.tile([P, PW], F32, name="picked"), bank)
 
         def capped(s, half, picked_t):
             nc.vector.tensor_tensor(
@@ -193,35 +210,39 @@ def tile_list_stamp_auction_search_kernel(
                 MIN,
             )
 
-        h = reading(0, w_first, first_cols)
         last = SLICES - 1
+        h = new([P, S], F32, "h")
+        for i, cols in enumerate(halves):
+            read = once.tile([P, NB], F32, name="read%d" % i, align_bytes=64)
+            tanh_part(0, cols, read[:])
+            nc.vector.tensor_tensor(h[:, cols], sum_part(w_first, first_cols, cols)[:], read[:], MULT)
+        nc.vector.tensor_tensor(pages[0][:].indirect(idx3[:]), h[:], wg[:], MULT)
+        picked_t = [pick_whole(0, turn_bank([P, PW // P, P]))]
 
-        def turn_caps(s):
+        weighted = [weighted_read(1)]
+        rest_bf16 = once.tile([P, len(w_passes), (H - P) * PACK], BF16, name="read1", align_bytes=64)
+        w_rest = quantize_weights(raw_rest, [rest_bf16[:, a, :] for a in range(len(w_passes))], "w_rest")
+        v2_sc = new([P, S2], U8, "raw_rest0")
+        gather(v2_sc[:], tab2_sc[:], idx2[:])
+        v2_w = new([P, S2], U32, "raw_rest2")
+        gather(v2_w[:], tab2_w[:].bitcast(U32), idx2[:])
+        weighted = weighted + [weighted_read(s) for s in range(2, SLICES)]
+        sums = [copied_sum(s) for s in range(1, SLICES)]
+        for s in range(SLICES):
             bank = psum.tile([P, PW // P, P], F32, name="both")
             nc.scalar.copy(caps_t[:, s, :, :], turned(caps[:, s, :], bank)[:])
 
-        picked_t = None
-        for s in range(last):
-            nc.vector.tensor_tensor(pages[s][:].indirect(idx3[:]), h[:], wg[:], MULT)
-            if s == 0:
-                rest_bf16 = once.tile([P, len(w_passes), (H - P) * PACK], BF16, name="read1", align_bytes=64)
-                w_rest = quantize_weights(raw_rest, [rest_bf16[:, a, :] for a in range(len(w_passes))], "w_rest")
-                v2_sc = new([P, S2], U8, "raw_rest0")
-                gather(v2_sc[:], tab2_sc[:], idx2[:])
-                v2_w = new([P, S2], U32, "raw_rest2")
-                gather(v2_w[:], tab2_w[:].bitcast(U32), idx2[:])
-            else:
-                for half in range(2):
-                    capped(s - 1, half, picked_t[:, JB * half : JB * (half + 1), :])
-            h = reading(s + 1, w_rest, slice(P * s, P * (s + 1)))
-            turn_caps(s)
-            picked_t = pick(s, 0, once.tile([P, PW], F32, name="read1", align_bytes=64))
-        turn_caps(last)
-        nc.vector.tensor_tensor(pages[last][:].indirect(idx3[:]), h[:], wg[:], MULT)
-        picked_last = [pick(last, JB * half, new([P, XH], F32, "picked%d" % half)) for half in range(2)]
+        for s in range(1, SLICES):
+            nc.vector.tensor_tensor(pages[s][:].indirect(idx3[:]), sums[s - 1][:], weighted[s - 1][:], MULT)
+            if s < last:
+                picked_t.append(pick_whole(s, psum.tile([P, PW // P, P], F32, name="both")))
+        picked_last = [
+            pick(last, JB * half, new([P, XH], F32, "picked%d" % half), psum.tile([P, JB, P], F32, name="z"))
+            for half in range(2)
+        ]
         for half in range(2):
-            capped(last - 1, half, picked_t[:, JB * half : JB * (half + 1), :])
-        for half in range(2):
+            for s in range(last):
+                capped(s, half, picked_t[s][:, JB * half : JB * (half + 1), :])
             capped(last, half, picked_last[half][:])
 
         out_rows = out.rearrange("(b p) j -> p b j", p=P)

@@ -3,14 +3,20 @@ from contextlib import ExitStack
 import concourse.mybir as mybir
 from concourse.masks import make_identity
 
-T, S, K, KI, H, T2, PW, T3, S2 = 2048, 1024, 1024, 512, 512, 2048, 512, 2048, 1024
+T = 2048
+S = 1024
+K = 1024
+KI = 512
+H = 512
+PW = 512
+T3 = 2048
+S2 = 1024
 FLOPS = 2 * S * H * (2 * K + KI) + 2 * S2 * PW * H
 
 F32 = mybir.dt.float32
 BF16 = mybir.dt.bfloat16
 I32 = mybir.dt.int32
 U32 = mybir.dt.uint32
-U16 = mybir.dt.uint16
 U8 = mybir.dt.uint8
 FP8X4 = mybir.dt.float8_e4m3fn_x4
 FP4X4 = mybir.dt.float4_e2m1fn_x4
@@ -20,13 +26,18 @@ ACT = mybir.ActivationFunctionType
 
 P = 128
 PACK = 4
+K_PASS = P * PACK
 QUADS = 4
+PER_COLUMN = 16
 NB = 512
 SLICES = H // P
 XH = PW // 2
 JB = XH // P
 IMG_ROW = 8
 TAB2_ROW = 12
+TURN_BANKS = 4
+STORES = 2 * S2 // P // 2
+VECTOR_BANKS = 3
 
 
 def tile_list_stamp_auction_search_kernel(
@@ -87,7 +98,7 @@ def tile_list_stamp_auction_search_kernel(
             return quantized
 
         def turn_bank(shape):
-            return psum.tile(shape, F32, name="turn", bufs=4)
+            return psum.tile(shape, F32, name="turn", bufs=TURN_BANKS)
 
         def turned(src, dst):
             blocks = dst.shape[1]
@@ -102,7 +113,7 @@ def tile_list_stamp_auction_search_kernel(
         img_sc = zeroed(S, "img_sc")
         tab2_sc = zeroed(T3, "tab2_sc")
 
-        w_passes = [w1[0:512, :], w2, w1[512:1024, :]]
+        w_passes = [w1[0:K_PASS, :], w2, w1[K_PASS:K, :]]
         first_cols, rest_cols = slice(0, P), slice(P, H)
         page_rows = page0.rearrange("(s p) c -> s p c", p=P)
 
@@ -142,15 +153,15 @@ def tile_list_stamp_auction_search_kernel(
         gather(v_sc1[:], tab_sc[:, T : 2 * T], idx[:])
         v_w1 = new([P, S], U32, "v_w1")
         for n0 in range(0, S, NB):
-            gather(v_w1[:, n0 : n0 + NB], tab_w1[:].bitcast(U32), idx[:, n0 // 16 : (n0 + NB) // 16])
+            entries = idx[:, n0 // PER_COLUMN : (n0 + NB) // PER_COLUMN]
+            gather(v_w1[:, n0 : n0 + NB], tab_w1[:].bitcast(U32), entries)
 
         v = [(v_w0, v_sc0), (v_w1, v_sc1)]
         moving = [v[0], (img_w, img_sc[IMG_ROW:P, :]), v[1]]
+        lot_banks = [slice(n0, n0 + NB) for n0 in range(0, S, NB)]
 
-        halves = [slice(n0, n0 + NB) for n0 in range(0, S, NB)]
-
-        def tanh_part(s, cols, read):
-            z = psum.tile([P, NB], F32, name="z")
+        def tanh_part(s, cols, read, bank_name):
+            z = psum.tile([P, NB], F32, name=bank_name)
             for a in range(2):
                 nc.tensor.matmul_mx(
                     out=z[:],
@@ -180,41 +191,41 @@ def tile_list_stamp_auction_search_kernel(
         def weighted_read(s):
             read = new([P, S], F32, "read_s%d" % s)
             weighted = new([P, S], F32, "weighted%d" % s)
-            for cols in halves:
-                tanh_part(s, cols, read[:, cols])
+            for cols in lot_banks:
+                tanh_part(s, cols, read[:, cols], "both")
                 nc.gpsimd.tensor_tensor(weighted[:, cols], read[:, cols], wg[:, cols], MULT)
             return weighted
 
         def copied_sum(s):
             dst = new([P, S], F32, "sum%d" % s)
-            for cols in halves:
+            for cols in lot_banks:
                 nc.scalar.copy(dst[:, cols], sum_part(w_rest, slice(P * (s - 1), P * s), cols)[:])
             return dst
 
         caps_t = new([P, SLICES, PW // P, P], F32, "caps_t")
-        x_t = [new([P, JB, H], BF16, "x_t%d" % half) for half in range(2)]
 
         def pick(s, b0, picked, bank):
             blocks = bank.shape[1]
-            gather(picked[:], pages[s][:], idx4[:, P // 16 * b0 : P // 16 * (b0 + blocks)])
+            entries = idx4[:, P // PER_COLUMN * b0 : P // PER_COLUMN * (b0 + blocks)]
+            gather(picked[:], pages[s][:], entries)
             return turned(picked, bank)
 
         def pick_whole(s, bank):
             return pick(s, 0, ring.tile([P, PW], F32, name="picked"), bank)
 
-        def capped(s, half, picked_t):
+        def capped(s, half, turned_slots):
             nc.vector.tensor_tensor(
                 x_t[half][:, :, P * s : P * (s + 1)],
-                picked_t,
+                turned_slots,
                 caps_t[:, s, JB * half : JB * (half + 1), :],
                 MIN,
             )
 
         last = SLICES - 1
         h = new([P, S], F32, "h")
-        for i, cols in enumerate(halves):
+        for i, cols in enumerate(lot_banks):
             read = once.tile([P, NB], F32, name="read%d" % i, align_bytes=64)
-            tanh_part(0, cols, read[:])
+            tanh_part(0, cols, read[:], "z")
             nc.vector.tensor_tensor(h[:, cols], sum_part(w_first, first_cols, cols)[:], read[:], MULT)
         nc.vector.tensor_tensor(pages[0][:].indirect(idx3[:]), h[:], wg[:], MULT)
         picked_t = [pick_whole(0, turn_bank([P, PW // P, P]))]
@@ -236,6 +247,7 @@ def tile_list_stamp_auction_search_kernel(
             nc.vector.tensor_tensor(pages[s][:].indirect(idx3[:]), sums[s - 1][:], weighted[s - 1][:], MULT)
             if s < last:
                 picked_t.append(pick_whole(s, psum.tile([P, PW // P, P], F32, name="both")))
+        x_t = [new([P, JB, H], BF16, name) for name in ("sum2", "weighted2")]
         picked_last = [
             pick(last, JB * half, new([P, XH], F32, "picked%d" % half), psum.tile([P, JB, P], F32, name="z"))
             for half in range(2)
@@ -260,10 +272,10 @@ def tile_list_stamp_auction_search_kernel(
                 pairs[:].rearrange("p b u j -> p b j u"),
             )
             x_codes, x_scales = quantize(x[:], XH, "x_q%d" % half)
-            for pair in range(S2 // P // 2):
-                e = psum.tile([P, 2, XH], F32, name=("z", "both")[pair % 2])
+            for bank_i in range(S2 // P // 2):
+                e = psum.tile([P, 2, XH], F32, name=("z", "both")[bank_i % 2])
                 for u in range(2):
-                    lots = slice(P * (2 * pair + u), P * (2 * pair + u + 1))
+                    lots = slice(P * (2 * bank_i + u), P * (2 * bank_i + u + 1))
                     nc.tensor.matmul_mx(
                         out=e[:, u, :],
                         lhsT=v2_w[:, lots].bitcast(FP8X4),
@@ -273,11 +285,11 @@ def tile_list_stamp_auction_search_kernel(
                         start=True,
                         stop=True,
                     )
-                staged = ring.tile([P, 2, XH], F32, name="staged", bufs=8)
+                staged = ring.tile([P, 2, XH], F32, name="staged", bufs=STORES)
                 for u in range(2):
-                    g = gains[:, 2 * pair + u : 2 * pair + u + 1]
-                    if half == 1 and pair < 3:
+                    g = gains[:, 2 * bank_i + u : 2 * bank_i + u + 1]
+                    if half == 1 and bank_i < VECTOR_BANKS:
                         nc.vector.tensor_scalar(staged[:, u, :], e[:, u, :], g, None, MULT)
                     else:
                         nc.scalar.activation(staged[:, u, :], e[:, u, :], ACT.Copy, scale=g)
-                nc.sync.dma_start(out_rows[:, 2 * pair : 2 * pair + 2, cols], staged[:])
+                nc.sync.dma_start(out_rows[:, 2 * bank_i : 2 * bank_i + 2, cols], staged[:])

from contextlib import ExitStack

import concourse.mybir as mybir
from concourse.masks import make_identity

T = 2048
S = 1024
K = 1024
KI = 512
H = 512
PW = 512
T3 = 2048
S2 = 1024
FLOPS = 2 * S * H * (2 * K + KI) + 2 * S2 * PW * H

F32 = mybir.dt.float32
BF16 = mybir.dt.bfloat16
I32 = mybir.dt.int32
U32 = mybir.dt.uint32
U8 = mybir.dt.uint8
FP8X4 = mybir.dt.float8_e4m3fn_x4
FP4X4 = mybir.dt.float4_e2m1fn_x4
MULT = mybir.AluOpType.mult
MIN = mybir.AluOpType.min
ACT = mybir.ActivationFunctionType

P = 128
PACK = 4
K_PASS = P * PACK
QUADS = 4
PER_COLUMN = 16
NB = 512
SLICES = H // P
XH = PW // 2
JB = XH // P
IMG_ROW = 8
TAB2_ROW = 12
TURN_BANKS = 4
STORES = 2 * S2 // P // 2
VECTOR_BANKS = 3


def tile_list_stamp_auction_search_kernel(
    tc, tab_words, tab_scales, offs, img_words, img_scales, w1, w2, w3_words, w3_scales, b3,
    page0, wgs, offs3, offs4, cap, tab2_words, tab2_scales, offs2, gain, out,
):
    nc = tc.nc
    with ExitStack() as ctx:
        keep = ctx.enter_context(tc.tile_pool(name="keep", bufs=1))
        ring = ctx.enter_context(tc.tile_pool(name="ring", bufs=2))
        once = ctx.enter_context(tc.tile_pool(name="once", bufs=1))
        psum = ctx.enter_context(tc.psum_pool(name="psum", bufs=2))

        def new(shape, dtype, name):
            return keep.tile(shape, dtype, name=name, align_bytes=64)

        def load(src, name):
            dst = new(list(src.shape), src.dtype, name)
            nc.sync.dma_start(dst[:], src)
            return dst

        def load_words(src, name):
            return load(src.rearrange("p c i -> p (c i)").bitcast(I32), name)

        def zeroed(width, name):
            dst = new([P, width], U8, name)
            nc.vector.memset(dst[:].bitcast(I32), 0)
            return dst

        def load_scales(dst, src, row):
            for q in range(QUADS):
                rows = dst[32 * q + row : 32 * q + row + 4, :].bitcast(I32)
                nc.sync.dma_start(
                    rows.rearrange("r (a n) -> r a n", a=src.shape[0]),
                    src[:, 4 * q : 4 * q + 4, :].bitcast(I32).rearrange("a r n -> r a n"),
                )

        def gather(dst, window, offsets):
            nc.vector.tensor_copy(dst, window.indirect(offsets))

        def quantize(src, width, name):
            codes = new([P, width], U32, name + "_codes")
            scales = new([P, width], U8, name + "_scales")
            nc.vector.quantize_mx(out=codes[:].bitcast(FP8X4), scales=scales[:], in_=src)
            return codes, scales

        def load_weight(rows, cols, name):
            return load(rows.rearrange("(p i) c -> p i c", i=PACK)[:, :, cols], name)

        def quantize_weights(raws, rounded, name):
            quantized = []
            for a, raw in enumerate(raws):
                nc.scalar.copy(
                    rounded[a].rearrange("p (c i) -> p c i", i=PACK),
                    raw[:].rearrange("p i c -> p c i"),
                )
                quantized.append(quantize(rounded[a], raw.shape[2], "%s%d" % (name, a)))
            return quantized

        def turn_bank(shape):
            return psum.tile(shape, F32, name="turn", bufs=TURN_BANKS)

        def turned(src, dst):
            blocks = dst.shape[1]
            for b in range(blocks):
                nc.tensor.transpose(dst[:, b, :], src[:, P * b : P * (b + 1)], ident[:])
            return dst

        ident = new([P, P], F32, "ident")
        make_identity(nc, ident[:])
        tab_sc = zeroed(2 * T, "tab_sc")
        w3_sc = zeroed(2 * H, "w3_sc")
        img_sc = zeroed(S, "img_sc")
        tab2_sc = zeroed(T3, "tab2_sc")

        w_passes = [w1[0:K_PASS, :], w2, w1[K_PASS:K, :]]
        first_cols, rest_cols = slice(0, P), slice(P, H)
        page_rows = page0.rearrange("(s p) c -> s p c", p=P)

        idx = load(offs, "idx")
        tab_w0 = load_words(tab_words[0], "tab_w0")
        load_scales(tab_sc, tab_scales, 0)
        raw_first = [load_weight(w_passes[a], first_cols, "raw_first%d" % a) for a in range(2)]
        w3_w = load(w3_words.rearrange("a p n -> p a n").bitcast(I32), "w3_w")
        load_scales(w3_sc, w3_scales, 0)
        raw_first.append(load_weight(w_passes[2], first_cols, "raw_first2"))
        tab_w1 = load_words(tab_words[1], "tab_w1")
        img_w = load_words(img_words[0], "img_w")
        with nc.allow_non_contiguous_dma(reason="one value a partition"):
            bias = load(b3.rearrange("(s p) -> p s", p=P), "bias")
        load_scales(img_sc, img_scales, IMG_ROW)
        wg = load(wgs, "wg")
        pages = [load(page_rows[0], "page0")]
        idx3 = load(offs3, "idx3")
        idx4 = load(offs4, "idx4")
        idx2 = load(offs2, "idx2")
        raw_rest = [load_weight(rows, rest_cols, "raw_rest%d" % a) for a, rows in enumerate(w_passes)]
        load_scales(tab2_sc, tab2_scales, TAB2_ROW)
        tab2_w = load_words(tab2_words[0], "tab2_w")
        caps = load(cap.rearrange("(s p) j -> p s j", p=P), "caps")
        for s in range(1, SLICES):
            pages.append(load(page_rows[s], "page%d" % s))
        with nc.allow_non_contiguous_dma(reason="one value a partition"):
            gains = load(gain.rearrange("(b p) -> p b", p=P), "gains")

        v_w0 = new([P, S], U32, "v_w0")
        gather(v_w0[:], tab_w0[:].bitcast(U32), idx[:])
        v_sc0 = new([P, S], U8, "v_sc0")
        gather(v_sc0[:], tab_sc[:, 0:T], idx[:])
        first_bf16 = [new([P, P * PACK], BF16, "first_bf16_%d" % a)[:] for a in range(len(w_passes))]
        w_first = quantize_weights(raw_first, first_bf16, "w_first")
        v_sc1 = new([P, S], U8, "first_bf16_1")
        gather(v_sc1[:], tab_sc[:, T : 2 * T], idx[:])
        v_w1 = new([P, S], U32, "v_w1")
        for n0 in range(0, S, NB):
            entries = idx[:, n0 // PER_COLUMN : (n0 + NB) // PER_COLUMN]
            gather(v_w1[:, n0 : n0 + NB], tab_w1[:].bitcast(U32), entries)

        v = [(v_w0, v_sc0), (v_w1, v_sc1)]
        moving = [v[0], (img_w, img_sc[IMG_ROW:P, :]), v[1]]
        lot_banks = [slice(n0, n0 + NB) for n0 in range(0, S, NB)]

        def tanh_part(s, cols, read, bank_name):
            z = psum.tile([P, NB], F32, name=bank_name)
            for a in range(2):
                nc.tensor.matmul_mx(
                    out=z[:],
                    lhsT=w3_w[:, a, P // 2 * s : P // 2 * (s + 1)].bitcast(FP4X4),
                    lhsT_scale=w3_sc[:, H * a + P * s : H * a + P * (s + 1)],
                    rhs=v[a][0][:, cols].bitcast(FP8X4),
                    rhs_scale=v[a][1][:, cols],
                    start=(a == 0),
                    stop=(a == 1),
                )
            nc.scalar.activation(read, z[:], ACT.Tanh, bias=bias[:, s : s + 1])

        def sum_part(weights, w_cols, cols):
            both = psum.tile([P, NB], F32, name="both")
            for a in range(len(moving)):
                nc.tensor.matmul_mx(
                    out=both[:],
                    lhsT=weights[a][0][:, w_cols].bitcast(FP8X4),
                    lhsT_scale=weights[a][1][:, w_cols],
                    rhs=moving[a][0][:, cols].bitcast(FP8X4),
                    rhs_scale=moving[a][1][:, cols],
                    start=(a == 0),
                    stop=(a == len(moving) - 1),
                )
            return both

        def weighted_read(s):
            read = new([P, S], F32, "read_s%d" % s)
            weighted = new([P, S], F32, "weighted%d" % s)
            for cols in lot_banks:
                tanh_part(s, cols, read[:, cols], "both")
                nc.gpsimd.tensor_tensor(weighted[:, cols], read[:, cols], wg[:, cols], MULT)
            return weighted

        def copied_sum(s):
            dst = new([P, S], F32, "sum%d" % s)
            for cols in lot_banks:
                nc.scalar.copy(dst[:, cols], sum_part(w_rest, slice(P * (s - 1), P * s), cols)[:])
            return dst

        caps_t = new([P, SLICES, PW // P, P], F32, "caps_t")

        def pick(s, b0, picked, bank):
            blocks = bank.shape[1]
            entries = idx4[:, P // PER_COLUMN * b0 : P // PER_COLUMN * (b0 + blocks)]
            gather(picked[:], pages[s][:], entries)
            return turned(picked, bank)

        def pick_whole(s, bank):
            return pick(s, 0, ring.tile([P, PW], F32, name="picked"), bank)

        def capped(s, half, turned_slots):
            nc.vector.tensor_tensor(
                x_t[half][:, :, P * s : P * (s + 1)],
                turned_slots,
                caps_t[:, s, JB * half : JB * (half + 1), :],
                MIN,
            )

        last = SLICES - 1
        h = new([P, S], F32, "h")
        for i, cols in enumerate(lot_banks):
            read = once.tile([P, NB], F32, name="read%d" % i, align_bytes=64)
            tanh_part(0, cols, read[:], "z")
            nc.vector.tensor_tensor(h[:, cols], sum_part(w_first, first_cols, cols)[:], read[:], MULT)
        nc.vector.tensor_tensor(pages[0][:].indirect(idx3[:]), h[:], wg[:], MULT)
        picked_t = [pick_whole(0, turn_bank([P, PW // P, P]))]

        weighted = [weighted_read(1)]
        rest_bf16 = once.tile([P, len(w_passes), (H - P) * PACK], BF16, name="read1", align_bytes=64)
        w_rest = quantize_weights(raw_rest, [rest_bf16[:, a, :] for a in range(len(w_passes))], "w_rest")
        v2_sc = new([P, S2], U8, "raw_rest0")
        gather(v2_sc[:], tab2_sc[:], idx2[:])
        v2_w = new([P, S2], U32, "raw_rest2")
        gather(v2_w[:], tab2_w[:].bitcast(U32), idx2[:])
        weighted = weighted + [weighted_read(s) for s in range(2, SLICES)]
        sums = [copied_sum(s) for s in range(1, SLICES)]
        for s in range(SLICES):
            bank = psum.tile([P, PW // P, P], F32, name="both")
            nc.scalar.copy(caps_t[:, s, :, :], turned(caps[:, s, :], bank)[:])

        for s in range(1, SLICES):
            nc.vector.tensor_tensor(pages[s][:].indirect(idx3[:]), sums[s - 1][:], weighted[s - 1][:], MULT)
            if s < last:
                picked_t.append(pick_whole(s, psum.tile([P, PW // P, P], F32, name="both")))
        x_t = [new([P, JB, H], BF16, name) for name in ("sum2", "weighted2")]
        picked_last = [
            pick(last, JB * half, new([P, XH], F32, "picked%d" % half), psum.tile([P, JB, P], F32, name="z"))
            for half in range(2)
        ]
        for half in range(2):
            for s in range(last):
                capped(s, half, picked_t[s][:, JB * half : JB * (half + 1), :])
            capped(last, half, picked_last[half][:])

        out_rows = out.rearrange("(b p) j -> p b j", p=P)
        for half in range(2):
            cols = slice(XH * half, XH * (half + 1))
            pairs = turn_bank([P, JB, 2, P])
            for b in range(JB):
                words = x_t[half][:, b, :].bitcast(F32)
                for u in range(2):
                    nc.tensor.transpose(pairs[:, b, u, :], words[:, u : H // 2 : 2], ident[:])
            x = new([P, XH * PACK], BF16, "x%d" % half)
            weave = nc.scalar.copy if half == 0 else nc.vector.tensor_copy
            weave(
                x[:].bitcast(F32).rearrange("p (b j u) -> p b j u", b=JB, u=2),
                pairs[:].rearrange("p b u j -> p b j u"),
            )
            x_codes, x_scales = quantize(x[:], XH, "x_q%d" % half)
            for bank_i in range(S2 // P // 2):
                e = psum.tile([P, 2, XH], F32, name=("z", "both")[bank_i % 2])
                for u in range(2):
                    lots = slice(P * (2 * bank_i + u), P * (2 * bank_i + u + 1))
                    nc.tensor.matmul_mx(
                        out=e[:, u, :],
                        lhsT=v2_w[:, lots].bitcast(FP8X4),
                        lhsT_scale=v2_sc[TAB2_ROW:P, lots],
                        rhs=x_codes[:].bitcast(FP8X4),
                        rhs_scale=x_scales[:],
                        start=True,
                        stop=True,
                    )
                staged = ring.tile([P, 2, XH], F32, name="staged", bufs=STORES)
                for u in range(2):
                    g = gains[:, 2 * bank_i + u : 2 * bank_i + u + 1]
                    if half == 1 and bank_i < VECTOR_BANKS:
                        nc.vector.tensor_scalar(staged[:, u, :], e[:, u, :], g, None, MULT)
                    else:
                        nc.scalar.activation(staged[:, u, :], e[:, u, :], ACT.Copy, scale=g)
                nc.sync.dma_start(out_rows[:, 2 * bank_i : 2 * bank_i + 2, cols], staged[:])
